import numpy as np
import ml_dtypes


def mxq(x, axis, fmt="e4m3"):
    dtype, down = {"e4m3": (ml_dtypes.float8_e4m3fn, 7), "e5m2": (ml_dtypes.float8_e5m2, 14)}[fmt]
    v = np.moveaxis(np.asarray(x, np.float32).astype(ml_dtypes.bfloat16).astype(np.float64), axis, -1)
    blocks = v.reshape(v.shape[:-1] + (-1, 32))
    amax = np.abs(blocks).max(-1, keepdims=True)
    byte = np.maximum(np.where(amax > 0, np.frexp(amax)[1] - 1 + 127, 0) - down, 1)
    scale = np.exp2(byte - 127.0)
    codes = (blocks / scale).astype(np.float32).astype(dtype).astype(np.float64)
    return np.moveaxis((codes * scale).reshape(v.shape), -1, axis)


WIDE = False


def mx_kscale(k):
    if not WIDE:
        return np.ones(k)
    levels = np.array([10, -10, 5, -5, 0])
    if k % 512:
        return np.exp2(np.random.permutation(np.resize(levels, k // 32))).repeat(32)
    a = np.empty((k // 512, 16))
    for p in range(k // 512):
        a[p, :8] = np.random.permutation(np.resize(levels, 8))
        for g in range(8):
            far = levels[np.abs(levels - a[p, g]) >= 10]
            a[p, g + 8] = far[np.random.randint(len(far))]
    return np.exp2(a.ravel()).repeat(32)


def f64(x):
    return np.asarray(x).astype(np.float64)


def striped(idx):
    return np.tile(idx.reshape(-1, 16).T, (8, 1)).astype(np.uint16)


def unstriped(offs):
    return offs[:16].T.reshape(-1).astype(np.int64)


E2M1 = np.array([0.0, 0.5, 1.0, 1.5, 2.0, 3.0, 4.0, 6.0, -0.0, -0.5, -1.0, -1.5, -2.0, -3.0, -4.0, -6.0])


def pack_weight(w, fmt):
    k, n = w.shape
    w = f64(np.asarray(w, np.float32).astype(ml_dtypes.bfloat16)).reshape(k // 32, 32, n)
    amax = np.abs(w).max(1)
    if fmt == "e4m3":
        byte = np.frexp(amax)[1] - 1 + 127 - 7
    else:
        mant, ex = np.frexp(amax / 6.0)
        byte = np.where(mant > 0.5, ex, ex - 1) + 127
    byte = np.clip(np.where(amax > 0, byte, 1), 1, 254)
    scaled = (w * np.exp2(127.0 - byte)[:, None, :]).reshape(k, n).astype(np.float32)
    by_word = np.ascontiguousarray(scaled.reshape(k // 512, 128, 4, n).transpose(0, 1, 3, 2))
    if fmt == "e4m3":
        words = by_word.astype(ml_dtypes.float8_e4m3fn).view(np.uint8)
    else:
        c = by_word.astype(ml_dtypes.float4_e2m1fn).view(np.uint8) & 0xF
        words = (c[..., 0::2] | (c[..., 1::2] << 4)).reshape(k // 512, 128, 2 * n)
    return np.ascontiguousarray(words), np.ascontiguousarray(byte.astype(np.uint8).reshape(k // 512, 16, n))


def unpack_weight(words, scales, fmt):
    g, _, n = scales.shape
    words = np.ascontiguousarray(words).reshape(g, 128, n, -1)
    if fmt == "e4m3":
        vals = words.view(ml_dtypes.float8_e4m3fn).astype(np.float64)
    else:
        nib = np.empty((g, 128, n, 4), np.uint8)
        nib[..., 0::2] = words & 0xF
        nib[..., 1::2] = words >> 4
        vals = E2M1[nib]
    vals = vals * np.repeat(np.exp2(scales.astype(np.float64) - 127.0), 8, axis=1)[..., None]
    return vals.transpose(0, 1, 3, 2).reshape(g * 512, n)


def sigmoid(v):
    return 1.0 / (1.0 + np.exp(-np.maximum(v, -700.0)))


K, T, E, C, H, N = 512, 640, 8, 128, 512, 512
TOP = 3
PAD = 64


def by_expert(wq, xq):
    return np.concatenate([wq[e].T @ xq[:, e * C:(e + 1) * C] for e in range(E)], axis=1)


def setup_inputs():
    n = np.random.standard_normal
    s = mx_kscale(K)[:, None]
    u = mx_kscale(H)
    slot_token = np.empty(E * C, np.int64); pos = np.tile(E * C + np.arange(T) % PAD, (TOP, 1)); taken = np.zeros(T, np.int64)
    liked = np.random.randn(T)
    for e in np.random.permutation(E):
        free = np.flatnonzero(taken < TOP); pick = np.random.permutation(free[np.argsort(-(liked[free] + np.random.gumbel(size=free.size)))[:C]]); slot_token[e * C:(e + 1) * C] = pick
        pos[taken[pick], pick] = e * C + np.arange(C); taken[pick] += 1
    g = np.random.uniform(0.2, 0.8, (TOP, T))
    w1 = [pack_weight(m, "e2m1") for m in n((E, K, H)) / np.sqrt(K) / s[None]]
    w3 = [pack_weight(m, "e2m1") for m in n((E, K, H)) / np.sqrt(K) / s[None] * u[None, None, :]]
    w2 = [pack_weight(m, "e2m1") for m in n((E, H, N)) / np.sqrt(H) / u[None, :, None]]
    return {
        "xT": (n((K, T)) * s).astype(np.float32),
        "w1_words": np.stack([m[0] for m in w1]),
        "w1_scales": np.stack([m[1] for m in w1]),
        "w3_words": np.stack([m[0] for m in w3]),
        "w3_scales": np.stack([m[1] for m in w3]),
        "w2_words": np.stack([m[0] for m in w2]),
        "w2_scales": np.stack([m[1] for m in w2]),
        "gate": np.stack([np.tile(r, (N, 1)) for r in g]).astype(np.float32),
        "offs": striped(slot_token),
        "pos1": striped(pos[0]),
        "pos2": striped(pos[1]),
        "pos3": striped(pos[2]),
    }


def reference(xT, w1_words, w1_scales, w3_words, w3_scales, w2_words, w2_scales, gate, offs, pos1, pos2, pos3):
    idx = unstriped(offs)
    w1 = np.stack([unpack_weight(w1_words[e], w1_scales[e], "e2m1") for e in range(E)])
    w3 = np.stack([unpack_weight(w3_words[e], w3_scales[e], "e2m1") for e in range(E)])
    w2 = np.stack([unpack_weight(w2_words[e], w2_scales[e], "e2m1") for e in range(E)])
    xq = mxq(f64(xT)[:, idx], 0, "e4m3")
    h = sigmoid(by_expert(w1, xq))
    h = h * by_expert(w3, xq)
    y = by_expert(w2, mxq(h, 0, "e4m3"))
    y = np.concatenate([y, np.zeros((N, PAD))], axis=1)
    return sum(f64(gate[r]) * y[:, unstriped(p)] for r, p in enumerate((pos1, pos2, pos3)))

@@ -1,0 +1,260 @@
+from contextlib import ExitStack
+
+import concourse.mybir as mybir
+from concourse.masks import make_identity
+
+K, T, E, C, H, N = 512, 640, 8, 128, 512, 512
+TOP = 3
+PAD = 64
+SLOTS = E * C
+FLOPS = 2 * SLOTS * (2 * K * H + H * N)
+
+P = 128
+PACK = 4
+F32 = mybir.dt.float32
+BF16 = mybir.dt.bfloat16
+I32 = mybir.dt.int32
+U32 = mybir.dt.uint32
+U16 = mybir.dt.uint16
+U8 = mybir.dt.uint8
+FP8X4 = mybir.dt.float8_e4m3fn_x4
+FP4X4 = mybir.dt.float4_e2m1fn_x4
+MULT = mybir.AluOpType.mult
+ADD = mybir.AluOpType.add
+SIGMOID = mybir.ActivationFunctionType.Sigmoid
+
+TOKEN_CHUNKS = ((0, 256), (256, 512), (512, 640))
+GATHER_GROUPS = ((0, 1), (1, 3), (3, 6), (6, 8))
+HIDDEN_GROUPS = ((0, 2), (2, 4), (4, 6), (6, 7), (7, 8))
+BANK_SETS = 3
+HALF = E // 2
+N_TILES = N // P
+T_BLOCKS = T // P
+
+
+def tile_moe_ecr_glu_sigmoid_kernel(
+    tc, xT, w1_words, w1_scales, w3_words, w3_scales, w2_words, w2_scales, gate, offs, pos1, pos2, pos3, out
+):
+    nc = tc.nc
+    with ExitStack() as ctx:
+        keep = ctx.enter_context(tc.tile_pool(name="keep", bufs=1))
+        ring = ctx.enter_context(tc.tile_pool(name="ring", bufs=2))
+        psum = ctx.enter_context(tc.psum_pool(name="psum", bufs=1))
+
+        def bank(tag, shape):
+            return psum.tile(shape, F32, name=tag, tag=tag)
+
+        def plane(name, experts, width):
+            t = keep.tile([P, experts, width], U8, name=name, align_bytes=64)
+            return t
+
+        def load_words(dst, words, e0, e1, c0, c1):
+            src = words.rearrange("e s p c -> p (e s) c")[:, e0:e1, c0:c1]
+            nc.sync.dma_start(out=dst.bitcast(I32), in_=src.bitcast(I32))
+
+        def load_scales(dst, scales, e0, e1, c0, c1):
+            rows = scales.rearrange("e s (q r) n -> r q (e s) n", r=4)
+            for r in range(4):
+                nc.sync.dma_start(out=dst[r:P:32, :, :].bitcast(I32), in_=rows[r][:, e0:e1, c0:c1].bitcast(I32))
+
+        offs_sb = keep.tile([P, SLOTS // 16], U16, name="offs_sb")
+        pos_sb = [keep.tile([P, T // 16], U16, name=f"pos_sb{r}") for r in range(TOP)]
+        s1 = [plane(f"s1_{h}", HALF, H) for h in range(2)]
+        s3 = [plane(f"s3_{h}", HALF, H) for h in range(2)]
+        s2_first = plane("s2_first", E, P)
+        s2_rest = plane("s2_rest", E, N - P)
+        w1 = keep.tile([P, E, 2 * H], U8, name="w1", align_bytes=64)
+        w3 = keep.tile([P, E, 2 * H], U8, name="w3", align_bytes=64)
+        w2_first = keep.tile([P, E, 2 * P], U8, name="w2_first", align_bytes=64)
+        y = [keep.tile([P, SLOTS + PAD], F32, name=f"y{nt}") for nt in range(N_TILES)]
+        tok_codes = keep.tile([P, T], U32, name="tok_codes", align_bytes=64)
+        tok_scales = keep.tile([P, T], U8, name="tok_scales", align_bytes=64)
+        slot_codes = keep.tile([P, SLOTS], U32, name="slot_codes", align_bytes=64)
+        slot_scales = keep.tile([P, SLOTS], U8, name="slot_scales", align_bytes=64)
+        h_codes = keep.tile([P, SLOTS], U32, name="h_codes", align_bytes=64)
+        h_scales = keep.tile([P, SLOTS], U8, name="h_scales", align_bytes=64)
+        ident = keep.tile([P, P], F32, name="ident")
+        warm = keep.tile([P, 1], F32, name="warm")
+
+        nc.gpsimd.memset(s1[0][:].bitcast(I32), 0)
+        for t in (s3[0], s1[1], s3[1], s2_first, s2_rest):
+            nc.vector.memset(t[:].bitcast(I32), 0)
+        nc.gpsimd.memset(tok_scales[:], 0)
+        for nt in range(N_TILES):
+            nc.gpsimd.memset(y[nt][:, SLOTS:], 0.0)
+        make_identity(nc, ident[:])
+        nc.scalar.activation(out=warm[:], in_=y[0][:, SLOTS : SLOTS + 1], func=SIGMOID)
+
+        x_rows = xT.rearrange("(p j) t -> p j t", j=PACK)
+        x_raw = []
+        for t0, t1 in TOKEN_CHUNKS:
+            raw = keep.tile([P, PACK, t1 - t0], F32, name=f"x_raw{t0}", tag=f"raw{t0}", align_bytes=64)
+            nc.sync.dma_start(out=raw[:], in_=x_rows[:, :, t0:t1])
+            x_raw.append(raw)
+        nc.sync.dma_start(offs_sb[:], offs)
+
+        def load_first_layer(e0, e1):
+            load_words(w1[:, e0:e1, :], w1_words, e0, e1, 0, 2 * H)
+            load_words(w3[:, e0:e1, :], w3_words, e0, e1, 0, 2 * H)
+
+        def load_gate(nt):
+            nc.sync.dma_start(out=gate_sb[nt][:], in_=gate[:, nt * P : (nt + 1) * P, :].rearrange("r p t -> p r t"))
+
+        load_first_layer(0, 1)
+        load_scales(s1[0], w1_scales, 0, HALF, 0, H)
+        load_scales(s3[0], w3_scales, 0, HALF, 0, H)
+        load_first_layer(1, 2)
+        load_first_layer(2, 4)
+        load_scales(s1[1], w1_scales, HALF, E, 0, H)
+        load_scales(s3[1], w3_scales, HALF, E, 0, H)
+        load_first_layer(4, 6)
+        load_first_layer(6, 8)
+        load_scales(s2_first, w2_scales, 0, E, 0, P)
+        load_words(w2_first[:], w2_words, 0, E, 0, 2 * P)
+        for r, pos in enumerate((pos1, pos2, pos3)):
+            nc.sync.dma_start(pos_sb[r][:], pos)
+
+        for raw, (t0, t1) in zip(x_raw, TOKEN_CHUNKS):
+            grouped = keep.tile([P, t1 - t0, PACK], BF16, name=f"x_grouped{t0}", tag=f"grouped{t0}", align_bytes=64)
+            nc.vector.tensor_copy(
+                out=grouped[:].rearrange("p (c i) j -> p c j i", i=4),
+                in_=raw[:].rearrange("p j (c i) -> p c j i", i=4),
+            )
+            nc.vector.quantize_mx(
+                out=tok_codes[:, t0:t1].bitcast(FP8X4),
+                scales=tok_scales[:, t0:t1],
+                in_=grouped[:].rearrange("p t j -> p (t j)"),
+            )
+
+        gate_sb = [
+            keep.tile([P, TOP, T], F32, name=f"gate{nt}", tag=tag, align_bytes=64)
+            for nt, tag in enumerate(("raw0", "raw512", "grouped0", "grouped256"))
+        ]
+        w2_rest = keep.tile([P, E, 2 * (N - P)], U8, name="w2_rest", tag="raw256", align_bytes=64)
+        load_gate(0)
+        load_scales(s2_rest, w2_scales, 0, E, P, N)
+        load_words(w2_rest[:], w2_words, 0, E, 2 * P, 2 * N)
+        for nt in range(1, N_TILES):
+            load_gate(nt)
+
+        def gather_tokens(e0, e1):
+            cols = slice(e0 * C, e1 * C)
+            entries = offs_sb[:, e0 * C // 16 : e1 * C // 16]
+            nc.vector.tensor_copy(out=slot_codes[:, cols], in_=tok_codes[:].indirect(entries))
+            nc.vector.tensor_copy(out=slot_scales[:, cols], in_=tok_scales[:].indirect(entries))
+
+        def second_layer(acc, e, nt):
+            cols = slice(e * C, (e + 1) * C)
+            if nt == 0:
+                words, scales = w2_first[:, e, :], s2_first[:, e, :]
+            else:
+                words = w2_rest[:, e, 2 * P * (nt - 1) : 2 * P * nt]
+                scales = s2_rest[:, e, P * (nt - 1) : P * nt]
+            nc.tensor.matmul_mx(
+                out=acc,
+                lhsT=words.bitcast(FP4X4),
+                lhsT_scale=scales,
+                rhs=h_codes[:, cols].bitcast(FP8X4),
+                rhs_scale=h_scales[:, cols],
+                start=True,
+                stop=True,
+            )
+
+        def first_layer(e):
+            cols = slice(e * C, (e + 1) * C)
+            sums = []
+            for tag, words, scales in (("a", w1, s1), ("b", w3, s3)):
+                acc = bank(f"{tag}{e % BANK_SETS}", [P, H])
+                nc.tensor.matmul_mx(
+                    out=acc[:],
+                    lhsT=slot_codes[:, cols].bitcast(FP8X4),
+                    lhsT_scale=slot_scales[:, cols],
+                    rhs=words[:, e, :].bitcast(FP4X4),
+                    rhs_scale=scales[e // HALF][:, e % HALF, :],
+                    start=True,
+                    stop=True,
+                )
+                sums.append(acc[:].rearrange("c (p u d) -> c u p d", u=2, d=2))
+            sig = ring.tile([P, 2, P, 2], F32, name="sig", bufs=3)
+            nc.scalar.activation(out=sig[:], in_=sums[0], func=SIGMOID)
+            h = ring.tile([P, 2, P, 2], BF16, name="h", bufs=4)
+            nc.vector.tensor_tensor(out=h[:], in0=sums[1], in1=sig[:], op=MULT)
+            return h
+
+        def quantise_hidden(hidden, e0, e1, tag):
+            cols = slice(e0 * C, e1 * C)
+            turned = bank(tag, [P, e1 - e0, 2, C])
+            for e in range(e0, e1):
+                pairs = hidden[e][:].rearrange("c u p d -> c (u p d)").bitcast(F32)
+                for u in range(2):
+                    nc.tensor.transpose(turned[:, e - e0, u, :], pairs[:, u * P : (u + 1) * P], ident[:])
+            grouped = ring.tile([P, (e1 - e0) * C * PACK], BF16, name="h_grouped", align_bytes=64)
+            nc.scalar.copy(
+                out=grouped[:].bitcast(F32).rearrange("p (e c u) -> p e c u", c=C, u=2),
+                in_=turned[:].rearrange("p e u c -> p e c u"),
+            )
+            nc.vector.quantize_mx(out=h_codes[:, cols].bitcast(FP8X4), scales=h_scales[:, cols], in_=grouped[:])
+
+        def results_of(e0, e1, nt, tag):
+            acc = bank(tag, [P, (e1 - e0) * C])
+            for e in range(e0, e1):
+                second_layer(acc[:, (e - e0) * C : (e - e0 + 1) * C], e, nt)
+            nc.scalar.copy(out=y[nt][:, e0 * C : e1 * C], in_=acc[:])
+
+        for e0, e1 in GATHER_GROUPS[:2]:
+            gather_tokens(e0, e1)
+        first_tile_groups = {6: (0, 4, "b2"), 7: (4, 7, "a2"), 8: (7, 8, "a0")}
+        hidden = []
+        for e in range(E + 1):
+            if e < E:
+                hidden.append(first_layer(e))
+            if e < 2:
+                gather_tokens(*GATHER_GROUPS[2 + e])
+            for g, (e0, e1) in enumerate(HIDDEN_GROUPS):
+                if e1 == e:
+                    quantise_hidden(hidden, e0, e1, f"t{g % 2}")
+            if e in first_tile_groups:
+                e0, e1, tag = first_tile_groups[e]
+                results_of(e0, e1, 0, tag)
+
+        for nt, (late, early) in enumerate((("b1", "a0"), ("a1", "b1"), ("b0", "a1"))):
+            results_of(HALF, E, nt + 1, late)
+            results_of(0, HALF, nt + 1, early)
+
+        sum_banks = (("a0", "b1"), ("a1", "b0"), ("a0", "b1"))
+        back_banks = (("t0", "t1"), ("a2", "b2"), ("t0", "t1"))
+        for nt in range(N_TILES):
+            terms = []
+            result = keep.tile([P, T], F32, name=f"result{nt}")
+            for r in range(TOP):
+                term = ring.tile([P, T], F32, name=f"term{r}")
+                nc.vector.tensor_tensor(out=term[:], in0=y[nt][:].indirect(pos_sb[r][:]), in1=gate_sb[nt][:, r, :], op=MULT)
+                terms.append(term)
+                if nt == N_TILES - 1 and r == 1:
+                    partial = keep.tile([P, T], F32, name="partial")
+                    nc.vector.tensor_tensor(out=partial[:], in0=terms[0][:], in1=terms[1][:], op=ADD)
+            if nt == N_TILES - 1:
+                nc.vector.tensor_tensor(out=result[:], in0=partial[:], in1=terms[2][:], op=ADD)
+            else:
+                summed = ring.tile([P, T], F32, name="summed")
+                for (b0, b1), tag_s in zip(((0, 3), (3, 5)), sum_banks[nt]):
+                    cols = slice(b0 * P, b1 * P)
+                    acc = bank(tag_s, [P, (b1 - b0) * P])
+                    for b in range(b0, b1):
+                        for r in range(TOP):
+                            nc.tensor.matmul(
+                                acc[:, (b - b0) * P : (b - b0 + 1) * P],
+                                lhsT=terms[r][:, b * P : (b + 1) * P],
+                                rhs=ident[:],
+                                is_transpose=True,
+                                start=(r == 0),
+                                stop=(r == TOP - 1),
+                            )
+                    nc.scalar.copy(out=summed[:, cols], in_=acc[:])
+                for (b0, b1), tag_r in zip(((0, 3), (3, 5)), back_banks[nt]):
+                    cols = slice(b0 * P, b1 * P)
+                    back = bank(tag_r, [P, (b1 - b0) * P])
+                    for b in range(b0, b1):
+                        nc.tensor.transpose(back[:, (b - b0) * P : (b - b0 + 1) * P], summed[:, b * P : (b + 1) * P], ident[:])
+                    nc.scalar.copy(out=result[:, cols], in_=back[:])
+            nc.sync.dma_start(out=out[nt * P : (nt + 1) * P, :], in_=result[:])

@@ -21,13 +21,15 @@ FP8X4 = mybir.dt.float8_e4m3fn_x4
 FP4X4 = mybir.dt.float4_e2m1fn_x4
 MULT = mybir.AluOpType.mult
 ADD = mybir.AluOpType.add
+COPY = mybir.ActivationFunctionType.Copy
 SIGMOID = mybir.ActivationFunctionType.Sigmoid
 
 TOKEN_CHUNKS = ((0, 256), (256, 512), (512, 640))
-GATHER_GROUPS = ((0, 1), (1, 3), (3, 6), (6, 8))
+GATHER_GROUPS = ((0, 2), (2, 5), (5, 8))
+SCALAR_TOKENS = (256, 0, 64)
 HIDDEN_GROUPS = ((0, 2), (2, 4), (4, 6), (6, 7), (7, 8))
-BANK_SETS = 3
 HALF = E // 2
+LAST_SPLIT = 448
 N_TILES = N // P
 T_BLOCKS = T // P
 
@@ -59,8 +61,8 @@ def tile_moe_ecr_glu_sigmoid_kernel(
 
         offs_sb = keep.tile([P, SLOTS // 16], U16, name="offs_sb")
         pos_sb = [keep.tile([P, T // 16], U16, name=f"pos_sb{r}") for r in range(TOP)]
-        s1 = [plane(f"s1_{h}", HALF, H) for h in range(2)]
-        s3 = [plane(f"s3_{h}", HALF, H) for h in range(2)]
+        s1 = plane("s1", E, H)
+        s3 = plane("s3", E, H)
         s2_first = plane("s2_first", E, P)
         s2_rest = plane("s2_rest", E, N - P)
         w1 = keep.tile([P, E, 2 * H], U8, name="w1", align_bytes=64)
@@ -76,10 +78,8 @@ def tile_moe_ecr_glu_sigmoid_kernel(
         ident = keep.tile([P, P], F32, name="ident")
         warm = keep.tile([P, 1], F32, name="warm")
 
-        nc.gpsimd.memset(s1[0][:].bitcast(I32), 0)
-        for t in (s3[0], s1[1], s3[1], s2_first, s2_rest):
+        for t in (s1, s3, tok_scales, s2_first, s2_rest):
             nc.vector.memset(t[:].bitcast(I32), 0)
-        nc.gpsimd.memset(tok_scales[:], 0)
         for nt in range(N_TILES):
             nc.gpsimd.memset(y[nt][:, SLOTS:], 0.0)
         make_identity(nc, ident[:])
@@ -101,25 +101,25 @@ def tile_moe_ecr_glu_sigmoid_kernel(
             nc.sync.dma_start(out=gate_sb[nt][:], in_=gate[:, nt * P : (nt + 1) * P, :].rearrange("r p t -> p r t"))
 
         load_first_layer(0, 1)
-        load_scales(s1[0], w1_scales, 0, HALF, 0, H)
-        load_scales(s3[0], w3_scales, 0, HALF, 0, H)
-        load_first_layer(1, 2)
-        load_first_layer(2, 4)
-        load_scales(s1[1], w1_scales, HALF, E, 0, H)
-        load_scales(s3[1], w3_scales, HALF, E, 0, H)
-        load_first_layer(4, 6)
-        load_first_layer(6, 8)
+        load_scales(s1, w1_scales, 0, E, 0, H)
+        load_scales(s3, w3_scales, 0, E, 0, H)
+        load_first_layer(1, 3)
+        load_first_layer(3, 5)
+        load_first_layer(5, 8)
         load_scales(s2_first, w2_scales, 0, E, 0, P)
         load_words(w2_first[:], w2_words, 0, E, 0, 2 * P)
         for r, pos in enumerate((pos1, pos2, pos3)):
             nc.sync.dma_start(pos_sb[r][:], pos)
 
-        for raw, (t0, t1) in zip(x_raw, TOKEN_CHUNKS):
+        for raw, (t0, t1), share in zip(x_raw, TOKEN_CHUNKS, SCALAR_TOKENS):
             grouped = keep.tile([P, t1 - t0, PACK], BF16, name=f"x_grouped{t0}", tag=f"grouped{t0}", align_bytes=64)
-            nc.vector.tensor_copy(
-                out=grouped[:].rearrange("p (c i) j -> p c j i", i=4),
-                in_=raw[:].rearrange("p j (c i) -> p c j i", i=4),
-            )
+            if share > 0:
+                nc.scalar.activation(out=grouped[:, :share, :], in_=raw[:, :, :share].rearrange("p j t -> p t j"), func=COPY)
+            if share < t1 - t0:
+                nc.vector.tensor_copy(
+                    out=grouped[:, share:, :].rearrange("p (c i) j -> p c j i", i=4),
+                    in_=raw[:, :, share:].rearrange("p j (c i) -> p c j i", i=4),
+                )
             nc.vector.quantize_mx(
                 out=tok_codes[:, t0:t1].bitcast(FP8X4),
                 scales=tok_scales[:, t0:t1],
@@ -163,21 +163,21 @@ def tile_moe_ecr_glu_sigmoid_kernel(
         def first_layer(e):
             cols = slice(e * C, (e + 1) * C)
             sums = []
-            for tag, words, scales in (("a", w1, s1), ("b", w3, s3)):
-                acc = bank(f"{tag}{e % BANK_SETS}", [P, H])
+            for tag, banks, words, scales in (("a", 2, w1, s1), ("b", 4, w3, s3)):
+                acc = bank(f"{tag}{e % banks}", [P, H])
                 nc.tensor.matmul_mx(
                     out=acc[:],
                     lhsT=slot_codes[:, cols].bitcast(FP8X4),
                     lhsT_scale=slot_scales[:, cols],
                     rhs=words[:, e, :].bitcast(FP4X4),
-                    rhs_scale=scales[e // HALF][:, e % HALF, :],
+                    rhs_scale=scales[:, e, :],
                     start=True,
                     stop=True,
                 )
                 sums.append(acc[:].rearrange("c (p u d) -> c u p d", u=2, d=2))
-            sig = ring.tile([P, 2, P, 2], F32, name="sig", bufs=3)
+            sig = ring.tile([P, 2, P, 2], F32, name="sig", bufs=4)
             nc.scalar.activation(out=sig[:], in_=sums[0], func=SIGMOID)
-            h = ring.tile([P, 2, P, 2], BF16, name="h", bufs=4)
+            h = ring.tile([P, 2, P, 2], BF16, name="h", bufs=5)
             nc.vector.tensor_tensor(out=h[:], in0=sums[1], in1=sig[:], op=MULT)
             return h
 
@@ -201,41 +201,51 @@ def tile_moe_ecr_glu_sigmoid_kernel(
                 second_layer(acc[:, (e - e0) * C : (e - e0 + 1) * C], e, nt)
             nc.scalar.copy(out=y[nt][:, e0 * C : e1 * C], in_=acc[:])
 
-        for e0, e1 in GATHER_GROUPS[:2]:
+        for e0, e1 in GATHER_GROUPS:
             gather_tokens(e0, e1)
-        first_tile_groups = {6: (0, 4, "b2"), 7: (4, 7, "a2"), 8: (7, 8, "a0")}
+        first_tile_groups = {7: (0, 4, "b0"), 8: (4, 7, "b1"), 9: (7, 8, "b2")}
         hidden = []
-        for e in range(E + 1):
+        for e in range(E + 2):
             if e < E:
                 hidden.append(first_layer(e))
-            if e < 2:
-                gather_tokens(*GATHER_GROUPS[2 + e])
             for g, (e0, e1) in enumerate(HIDDEN_GROUPS):
-                if e1 == e:
+                if e1 + 1 == e:
                     quantise_hidden(hidden, e0, e1, f"t{g % 2}")
             if e in first_tile_groups:
                 e0, e1, tag = first_tile_groups[e]
                 results_of(e0, e1, 0, tag)
 
-        for nt, (late, early) in enumerate((("b1", "a0"), ("a1", "b1"), ("b0", "a1"))):
+        for nt, (late, early) in enumerate((("b3", "b2"), ("a1", "b3"), ("a0", "a1"))):
             results_of(HALF, E, nt + 1, late)
             results_of(0, HALF, nt + 1, early)
 
-        sum_banks = (("a0", "b1"), ("a1", "b0"), ("a0", "b1"))
-        back_banks = (("t0", "t1"), ("a2", "b2"), ("t0", "t1"))
+        sum_banks = (("b2", "b3"), ("a1", "a0"), ("b2", "b3"))
+        back_banks = (("t0", "t1"), ("b0", "b1"), ("t0", "t1"))
         for nt in range(N_TILES):
-            terms = []
+            rows = slice(nt * P, (nt + 1) * P)
             result = keep.tile([P, T], F32, name=f"result{nt}")
-            for r in range(TOP):
-                term = ring.tile([P, T], F32, name=f"term{r}")
-                nc.vector.tensor_tensor(out=term[:], in0=y[nt][:].indirect(pos_sb[r][:]), in1=gate_sb[nt][:, r, :], op=MULT)
-                terms.append(term)
-                if nt == N_TILES - 1 and r == 1:
-                    partial = keep.tile([P, T], F32, name="partial")
-                    nc.vector.tensor_tensor(out=partial[:], in0=terms[0][:], in1=terms[1][:], op=ADD)
+            terms = [ring.tile([P, T], F32, name=f"term{r}") for r in range(TOP)]
+
+            def gated(r, t0, t1):
+                nc.vector.tensor_tensor(
+                    out=terms[r][:, t0:t1],
+                    in0=y[nt][:].indirect(pos_sb[r][:, t0 // 16 : t1 // 16]),
+                    in1=gate_sb[nt][:, r, t0:t1],
+                    op=MULT,
+                )
+
+            gated(0, 0, T)
+            gated(1, 0, T)
             if nt == N_TILES - 1:
-                nc.vector.tensor_tensor(out=result[:], in0=partial[:], in1=terms[2][:], op=ADD)
+                partial = keep.tile([P, T], F32, name="partial")
+                gated(2, 0, LAST_SPLIT)
+                nc.vector.tensor_tensor(out=partial[:], in0=terms[0][:], in1=terms[1][:], op=ADD)
+                gated(2, LAST_SPLIT, T)
+                for cols in (slice(0, LAST_SPLIT), slice(LAST_SPLIT, T)):
+                    nc.vector.tensor_tensor(out=result[:, cols], in0=partial[:, cols], in1=terms[2][:, cols], op=ADD)
+                    nc.sync.dma_start(out=out[rows, cols], in_=result[:, cols])
             else:
+                gated(2, 0, T)
                 summed = ring.tile([P, T], F32, name="summed")
                 for (b0, b1), tag_s in zip(((0, 3), (3, 5)), sum_banks[nt]):
                     cols = slice(b0 * P, b1 * P)
@@ -257,4 +267,4 @@ def tile_moe_ecr_glu_sigmoid_kernel(
                     for b in range(b0, b1):
                         nc.tensor.transpose(back[:, (b - b0) * P : (b - b0 + 1) * P], summed[:, b * P : (b + 1) * P], ident[:])
                     nc.scalar.copy(out=result[:, cols], in_=back[:])
-            nc.sync.dma_start(out=out[nt * P : (nt + 1) * P, :], in_=result[:])
+                nc.sync.dma_start(out=out[rows, :], in_=result[:])

from contextlib import ExitStack

import concourse.mybir as mybir
from concourse.masks import make_identity

K, T, E, C, H, N = 512, 640, 8, 128, 512, 512
TOP = 3
PAD = 64
SLOTS = E * C
FLOPS = 2 * SLOTS * (2 * K * H + H * N)

P = 128
PACK = 4
F32 = mybir.dt.float32
BF16 = mybir.dt.bfloat16
I32 = mybir.dt.int32
U32 = mybir.dt.uint32
U16 = mybir.dt.uint16
U8 = mybir.dt.uint8
FP8X4 = mybir.dt.float8_e4m3fn_x4
FP4X4 = mybir.dt.float4_e2m1fn_x4
MULT = mybir.AluOpType.mult
ADD = mybir.AluOpType.add
COPY = mybir.ActivationFunctionType.Copy
SIGMOID = mybir.ActivationFunctionType.Sigmoid

TOKEN_CHUNKS = ((0, 256), (256, 512), (512, 640))
GATHER_GROUPS = ((0, 2), (2, 5), (5, 8))
SCALAR_TOKENS = (256, 0, 64)
HIDDEN_GROUPS = ((0, 2), (2, 4), (4, 6), (6, 7), (7, 8))
HALF = E // 2
LAST_SPLIT = 448
N_TILES = N // P
T_BLOCKS = T // P


def tile_moe_ecr_glu_sigmoid_kernel(
    tc, xT, w1_words, w1_scales, w3_words, w3_scales, w2_words, w2_scales, gate, offs, pos1, pos2, pos3, out
):
    nc = tc.nc
    with ExitStack() as ctx:
        keep = ctx.enter_context(tc.tile_pool(name="keep", bufs=1))
        ring = ctx.enter_context(tc.tile_pool(name="ring", bufs=2))
        psum = ctx.enter_context(tc.psum_pool(name="psum", bufs=1))

        def bank(tag, shape):
            return psum.tile(shape, F32, name=tag, tag=tag)

        def plane(name, experts, width):
            t = keep.tile([P, experts, width], U8, name=name, align_bytes=64)
            return t

        def load_words(dst, words, e0, e1, c0, c1):
            src = words.rearrange("e s p c -> p (e s) c")[:, e0:e1, c0:c1]
            nc.sync.dma_start(out=dst.bitcast(I32), in_=src.bitcast(I32))

        def load_scales(dst, scales, e0, e1, c0, c1):
            rows = scales.rearrange("e s (q r) n -> r q (e s) n", r=4)
            for r in range(4):
                nc.sync.dma_start(out=dst[r:P:32, :, :].bitcast(I32), in_=rows[r][:, e0:e1, c0:c1].bitcast(I32))

        offs_sb = keep.tile([P, SLOTS // 16], U16, name="offs_sb")
        pos_sb = [keep.tile([P, T // 16], U16, name=f"pos_sb{r}") for r in range(TOP)]
        s1 = plane("s1", E, H)
        s3 = plane("s3", E, H)
        s2_first = plane("s2_first", E, P)
        s2_rest = plane("s2_rest", E, N - P)
        w1 = keep.tile([P, E, 2 * H], U8, name="w1", align_bytes=64)
        w3 = keep.tile([P, E, 2 * H], U8, name="w3", align_bytes=64)
        w2_first = keep.tile([P, E, 2 * P], U8, name="w2_first", align_bytes=64)
        y = [keep.tile([P, SLOTS + PAD], F32, name=f"y{nt}") for nt in range(N_TILES)]
        tok_codes = keep.tile([P, T], U32, name="tok_codes", align_bytes=64)
        tok_scales = keep.tile([P, T], U8, name="tok_scales", align_bytes=64)
        slot_codes = keep.tile([P, SLOTS], U32, name="slot_codes", align_bytes=64)
        slot_scales = keep.tile([P, SLOTS], U8, name="slot_scales", align_bytes=64)
        h_codes = keep.tile([P, SLOTS], U32, name="h_codes", align_bytes=64)
        h_scales = keep.tile([P, SLOTS], U8, name="h_scales", align_bytes=64)
        ident = keep.tile([P, P], F32, name="ident")
        warm = keep.tile([P, 1], F32, name="warm")

        for t in (s1, s3, tok_scales, s2_first, s2_rest):
            nc.vector.memset(t[:].bitcast(I32), 0)
        for nt in range(N_TILES):
            nc.gpsimd.memset(y[nt][:, SLOTS:], 0.0)
        make_identity(nc, ident[:])
        nc.scalar.activation(out=warm[:], in_=y[0][:, SLOTS : SLOTS + 1], func=SIGMOID)

        x_rows = xT.rearrange("(p j) t -> p j t", j=PACK)
        x_raw = []
        for t0, t1 in TOKEN_CHUNKS:
            raw = keep.tile([P, PACK, t1 - t0], F32, name=f"x_raw{t0}", tag=f"raw{t0}", align_bytes=64)
            nc.sync.dma_start(out=raw[:], in_=x_rows[:, :, t0:t1])
            x_raw.append(raw)
        nc.sync.dma_start(offs_sb[:], offs)

        def load_first_layer(e0, e1):
            load_words(w1[:, e0:e1, :], w1_words, e0, e1, 0, 2 * H)
            load_words(w3[:, e0:e1, :], w3_words, e0, e1, 0, 2 * H)

        def load_gate(nt):
            nc.sync.dma_start(out=gate_sb[nt][:], in_=gate[:, nt * P : (nt + 1) * P, :].rearrange("r p t -> p r t"))

        load_first_layer(0, 1)
        load_scales(s1, w1_scales, 0, E, 0, H)
        load_scales(s3, w3_scales, 0, E, 0, H)
        load_first_layer(1, 3)
        load_first_layer(3, 5)
        load_first_layer(5, 8)
        load_scales(s2_first, w2_scales, 0, E, 0, P)
        load_words(w2_first[:], w2_words, 0, E, 0, 2 * P)
        for r, pos in enumerate((pos1, pos2, pos3)):
            nc.sync.dma_start(pos_sb[r][:], pos)

        for raw, (t0, t1), share in zip(x_raw, TOKEN_CHUNKS, SCALAR_TOKENS):
            grouped = keep.tile([P, t1 - t0, PACK], BF16, name=f"x_grouped{t0}", tag=f"grouped{t0}", align_bytes=64)
            if share > 0:
                nc.scalar.activation(out=grouped[:, :share, :], in_=raw[:, :, :share].rearrange("p j t -> p t j"), func=COPY)
            if share < t1 - t0:
                nc.vector.tensor_copy(
                    out=grouped[:, share:, :].rearrange("p (c i) j -> p c j i", i=4),
                    in_=raw[:, :, share:].rearrange("p j (c i) -> p c j i", i=4),
                )
            nc.vector.quantize_mx(
                out=tok_codes[:, t0:t1].bitcast(FP8X4),
                scales=tok_scales[:, t0:t1],
                in_=grouped[:].rearrange("p t j -> p (t j)"),
            )

        gate_sb = [
            keep.tile([P, TOP, T], F32, name=f"gate{nt}", tag=tag, align_bytes=64)
            for nt, tag in enumerate(("raw0", "raw512", "grouped0", "grouped256"))
        ]
        w2_rest = keep.tile([P, E, 2 * (N - P)], U8, name="w2_rest", tag="raw256", align_bytes=64)
        load_gate(0)
        load_scales(s2_rest, w2_scales, 0, E, P, N)
        load_words(w2_rest[:], w2_words, 0, E, 2 * P, 2 * N)
        for nt in range(1, N_TILES):
            load_gate(nt)

        def gather_tokens(e0, e1):
            cols = slice(e0 * C, e1 * C)
            entries = offs_sb[:, e0 * C // 16 : e1 * C // 16]
            nc.vector.tensor_copy(out=slot_codes[:, cols], in_=tok_codes[:].indirect(entries))
            nc.vector.tensor_copy(out=slot_scales[:, cols], in_=tok_scales[:].indirect(entries))

        def second_layer(acc, e, nt):
            cols = slice(e * C, (e + 1) * C)
            if nt == 0:
                words, scales = w2_first[:, e, :], s2_first[:, e, :]
            else:
                words = w2_rest[:, e, 2 * P * (nt - 1) : 2 * P * nt]
                scales = s2_rest[:, e, P * (nt - 1) : P * nt]
            nc.tensor.matmul_mx(
                out=acc,
                lhsT=words.bitcast(FP4X4),
                lhsT_scale=scales,
                rhs=h_codes[:, cols].bitcast(FP8X4),
                rhs_scale=h_scales[:, cols],
                start=True,
                stop=True,
            )

        def first_layer(e):
            cols = slice(e * C, (e + 1) * C)
            sums = []
            for tag, banks, words, scales in (("a", 2, w1, s1), ("b", 4, w3, s3)):
                acc = bank(f"{tag}{e % banks}", [P, H])
                nc.tensor.matmul_mx(
                    out=acc[:],
                    lhsT=slot_codes[:, cols].bitcast(FP8X4),
                    lhsT_scale=slot_scales[:, cols],
                    rhs=words[:, e, :].bitcast(FP4X4),
                    rhs_scale=scales[:, e, :],
                    start=True,
                    stop=True,
                )
                sums.append(acc[:].rearrange("c (p u d) -> c u p d", u=2, d=2))
            sig = ring.tile([P, 2, P, 2], F32, name="sig", bufs=4)
            nc.scalar.activation(out=sig[:], in_=sums[0], func=SIGMOID)
            h = ring.tile([P, 2, P, 2], BF16, name="h", bufs=5)
            nc.vector.tensor_tensor(out=h[:], in0=sums[1], in1=sig[:], op=MULT)
            return h

        def quantise_hidden(hidden, e0, e1, tag):
            cols = slice(e0 * C, e1 * C)
            turned = bank(tag, [P, e1 - e0, 2, C])
            for e in range(e0, e1):
                pairs = hidden[e][:].rearrange("c u p d -> c (u p d)").bitcast(F32)
                for u in range(2):
                    nc.tensor.transpose(turned[:, e - e0, u, :], pairs[:, u * P : (u + 1) * P], ident[:])
            grouped = ring.tile([P, (e1 - e0) * C * PACK], BF16, name="h_grouped", align_bytes=64)
            nc.scalar.copy(
                out=grouped[:].bitcast(F32).rearrange("p (e c u) -> p e c u", c=C, u=2),
                in_=turned[:].rearrange("p e u c -> p e c u"),
            )
            nc.vector.quantize_mx(out=h_codes[:, cols].bitcast(FP8X4), scales=h_scales[:, cols], in_=grouped[:])

        def results_of(e0, e1, nt, tag):
            acc = bank(tag, [P, (e1 - e0) * C])
            for e in range(e0, e1):
                second_layer(acc[:, (e - e0) * C : (e - e0 + 1) * C], e, nt)
            nc.scalar.copy(out=y[nt][:, e0 * C : e1 * C], in_=acc[:])

        for e0, e1 in GATHER_GROUPS:
            gather_tokens(e0, e1)
        first_tile_groups = {7: (0, 4, "b0"), 8: (4, 7, "b1"), 9: (7, 8, "b2")}
        hidden = []
        for e in range(E + 2):
            if e < E:
                hidden.append(first_layer(e))
            for g, (e0, e1) in enumerate(HIDDEN_GROUPS):
                if e1 + 1 == e:
                    quantise_hidden(hidden, e0, e1, f"t{g % 2}")
            if e in first_tile_groups:
                e0, e1, tag = first_tile_groups[e]
                results_of(e0, e1, 0, tag)

        for nt, (late, early) in enumerate((("b3", "b2"), ("a1", "b3"), ("a0", "a1"))):
            results_of(HALF, E, nt + 1, late)
            results_of(0, HALF, nt + 1, early)

        sum_banks = (("b2", "b3"), ("a1", "a0"), ("b2", "b3"))
        back_banks = (("t0", "t1"), ("b0", "b1"), ("t0", "t1"))
        for nt in range(N_TILES):
            rows = slice(nt * P, (nt + 1) * P)
            result = keep.tile([P, T], F32, name=f"result{nt}")
            terms = [ring.tile([P, T], F32, name=f"term{r}") for r in range(TOP)]

            def gated(r, t0, t1):
                nc.vector.tensor_tensor(
                    out=terms[r][:, t0:t1],
                    in0=y[nt][:].indirect(pos_sb[r][:, t0 // 16 : t1 // 16]),
                    in1=gate_sb[nt][:, r, t0:t1],
                    op=MULT,
                )

            gated(0, 0, T)
            gated(1, 0, T)
            if nt == N_TILES - 1:
                partial = keep.tile([P, T], F32, name="partial")
                gated(2, 0, LAST_SPLIT)
                nc.vector.tensor_tensor(out=partial[:], in0=terms[0][:], in1=terms[1][:], op=ADD)
                gated(2, LAST_SPLIT, T)
                for cols in (slice(0, LAST_SPLIT), slice(LAST_SPLIT, T)):
                    nc.vector.tensor_tensor(out=result[:, cols], in0=partial[:, cols], in1=terms[2][:, cols], op=ADD)
                    nc.sync.dma_start(out=out[rows, cols], in_=result[:, cols])
            else:
                gated(2, 0, T)
                summed = ring.tile([P, T], F32, name="summed")
                for (b0, b1), tag_s in zip(((0, 3), (3, 5)), sum_banks[nt]):
                    cols = slice(b0 * P, b1 * P)
                    acc = bank(tag_s, [P, (b1 - b0) * P])
                    for b in range(b0, b1):
                        for r in range(TOP):
                            nc.tensor.matmul(
                                acc[:, (b - b0) * P : (b - b0 + 1) * P],
                                lhsT=terms[r][:, b * P : (b + 1) * P],
                                rhs=ident[:],
                                is_transpose=True,
                                start=(r == 0),
                                stop=(r == TOP - 1),
                            )
                    nc.scalar.copy(out=summed[:, cols], in_=acc[:])
                for (b0, b1), tag_r in zip(((0, 3), (3, 5)), back_banks[nt]):
                    cols = slice(b0 * P, b1 * P)
                    back = bank(tag_r, [P, (b1 - b0) * P])
                    for b in range(b0, b1):
                        nc.tensor.transpose(back[:, (b - b0) * P : (b - b0 + 1) * P], summed[:, b * P : (b + 1) * P], ident[:])
                    nc.scalar.copy(out=result[:, cols], in_=back[:])
                nc.sync.dma_start(out=out[rows, :], in_=result[:])
